import numpy as np
import ml_dtypes


def mxq(x, axis, fmt="e4m3"):
    dtype, down = {"e4m3": (ml_dtypes.float8_e4m3fn, 7), "e5m2": (ml_dtypes.float8_e5m2, 14)}[fmt]
    v = np.moveaxis(np.asarray(x, np.float32).astype(ml_dtypes.bfloat16).astype(np.float64), axis, -1)
    blocks = v.reshape(v.shape[:-1] + (-1, 32))
    amax = np.abs(blocks).max(-1, keepdims=True)
    byte = np.maximum(np.where(amax > 0, np.frexp(amax)[1] - 1 + 127, 0) - down, 1)
    scale = np.exp2(byte - 127.0)
    codes = (blocks / scale).astype(np.float32).astype(dtype).astype(np.float64)
    return np.moveaxis((codes * scale).reshape(v.shape), -1, axis)


WIDE = False


def mx_kscale(k):
    if not WIDE:
        return np.ones(k)
    levels = np.array([10, -10, 5, -5, 0])
    if k % 512:
        return np.exp2(np.random.permutation(np.resize(levels, k // 32))).repeat(32)
    a = np.empty((k // 512, 16))
    for p in range(k // 512):
        a[p, :8] = np.random.permutation(np.resize(levels, 8))
        for g in range(8):
            far = levels[np.abs(levels - a[p, g]) >= 10]
            a[p, g + 8] = far[np.random.randint(len(far))]
    return np.exp2(a.ravel()).repeat(32)


def f64(x):
    return np.asarray(x).astype(np.float64)


def striped(idx):
    return np.tile(idx.reshape(-1, 16).T, (8, 1)).astype(np.uint16)


def unstriped(offs):
    return offs[:16].T.reshape(-1).astype(np.int64)


E2M1 = np.array([0.0, 0.5, 1.0, 1.5, 2.0, 3.0, 4.0, 6.0, -0.0, -0.5, -1.0, -1.5, -2.0, -3.0, -4.0, -6.0])


def pack_weight(w, fmt):
    k, n = w.shape
    w = f64(np.asarray(w, np.float32).astype(ml_dtypes.bfloat16)).reshape(k // 32, 32, n)
    amax = np.abs(w).max(1)
    if fmt == "e4m3":
        byte = np.frexp(amax)[1] - 1 + 127 - 7
    else:
        mant, ex = np.frexp(amax / 6.0)
        byte = np.where(mant > 0.5, ex, ex - 1) + 127
    byte = np.clip(np.where(amax > 0, byte, 1), 1, 254)
    scaled = (w * np.exp2(127.0 - byte)[:, None, :]).reshape(k, n).astype(np.float32)
    by_word = np.ascontiguousarray(scaled.reshape(k // 512, 128, 4, n).transpose(0, 1, 3, 2))
    if fmt == "e4m3":
        words = by_word.astype(ml_dtypes.float8_e4m3fn).view(np.uint8)
    else:
        c = by_word.astype(ml_dtypes.float4_e2m1fn).view(np.uint8) & 0xF
        words = (c[..., 0::2] | (c[..., 1::2] << 4)).reshape(k // 512, 128, 2 * n)
    return np.ascontiguousarray(words), np.ascontiguousarray(byte.astype(np.uint8).reshape(k // 512, 16, n))


def unpack_weight(words, scales, fmt):
    g, _, n = scales.shape
    words = np.ascontiguousarray(words).reshape(g, 128, n, -1)
    if fmt == "e4m3":
        vals = words.view(ml_dtypes.float8_e4m3fn).astype(np.float64)
    else:
        nib = np.empty((g, 128, n, 4), np.uint8)
        nib[..., 0::2] = words & 0xF
        nib[..., 1::2] = words >> 4
        vals = E2M1[nib]
    vals = vals * np.repeat(np.exp2(scales.astype(np.float64) - 127.0), 8, axis=1)[..., None]
    return vals.transpose(0, 1, 3, 2).reshape(g * 512, n)


def silu(v):
    return v / (1.0 + np.exp(-np.maximum(v, -700.0)))


K, T, E, G, H, N = 512, 1024, 8, 2, 512, 512


def setup_inputs():
    n = np.random.standard_normal
    s = mx_kscale(K)
    u = mx_kscale(H)
    chosen = np.random.permutation(E)[:G]
    x = pack_weight(n((K, T)) * s[:, None], "e4m3")
    w1 = pack_weight(n((K, E * H)) / np.sqrt(K) / s[:, None] * np.tile(u, E), "e4m3")
    w2 = pack_weight(n((H, E * N)) / np.sqrt(H) / u[:, None], "e4m3")
    return {
        "x_words": x[0],
        "x_scales": x[1],
        "w1_words": w1[0],
        "w1_scales": w1[1],
        "w2_words": w2[0],
        "w2_scales": w2[1],
        "gate": np.stack([np.tile(r, (128, 1)) for r in np.random.uniform(0.2, 1.0, (G, T))]).astype(np.float32),
        "offs": striped((chosen[:, None] * H + np.arange(H)).reshape(-1)),
        "offs2": striped((chosen[:, None] * N + np.arange(N)).reshape(-1)),
    }


def reference(x_words, x_scales, w1_words, w1_scales, w2_words, w2_scales, gate, offs, offs2):
    idx, idx2 = unstriped(offs), unstriped(offs2)
    x = unpack_weight(x_words, x_scales, "e4m3")
    w1 = unpack_weight(w1_words, w1_scales, "e4m3")[:, idx]
    w2 = unpack_weight(w2_words, w2_scales, "e4m3")[:, idx2]
    y = np.zeros((N, T))
    for r in range(G):
        h = f64(gate[r, :1]) * silu(w1[:, r * H:(r + 1) * H].T @ x)
        y = y + w2[:, r * N:(r + 1) * N].T @ mxq(h, 0, "e4m3")
    return y

@@ -1,0 +1,209 @@
+from contextlib import ExitStack
+
+import concourse.mybir as mybir
+from concourse.masks import make_identity
+
+K, T, E, G, H, N = 512, 1024, 8, 2, 512, 512
+FLOPS = 2 * T * G * (K * H + H * N)
+BYTES = K * T + K * E * H + H * E * N + (K // 32) * (T + E * H + E * N) + 4 * G * T + 2 * 2 * 128 * 64 + 4 * N * T
+
+F32 = mybir.dt.float32
+BF16 = mybir.dt.bfloat16
+I32 = mybir.dt.int32
+U32 = mybir.dt.uint32
+U16 = mybir.dt.uint16
+U8 = mybir.dt.uint8
+FP8X4 = mybir.dt.float8_e4m3fn_x4
+SILU = mybir.ActivationFunctionType.Silu
+MULT = mybir.AluOpType.mult
+
+P = 128
+PACK = 4
+LIST_ROWS = 16
+TILES = T // P
+CHUNK = 256
+CHUNKS = T // CHUNK
+TPC = CHUNK // P
+W1_ROW, X_ROW, W2_ROW = 4, 8, 12
+
+
+def load_scales(queue, plane, scales, row):
+    rows = scales[0].bitcast(I32).rearrange("(q j) c -> j q c", j=4)
+    for j in range(4):
+        queue.dma_start(out=plane[:].bitcast(I32)[row + j : P : 32, :], in_=rows[j])
+
+
+def words_of(packed):
+    return packed[0].rearrange("p c d -> p (c d)").bitcast(I32)
+
+
+def tile_moe_wsel_b_silu_p_kernel(
+    tc, x_words, x_scales, w1_words, w1_scales, w2_words, w2_scales, gate, offs, offs2, out
+):
+    nc = tc.nc
+    with ExitStack() as ctx:
+        keep = ctx.enter_context(tc.tile_pool(name="keep", bufs=1))
+        work = ctx.enter_context(tc.tile_pool(name="work", bufs=1))
+        psum = ctx.enter_context(tc.psum_pool(name="psum", bufs=1))
+
+        list1 = keep.tile([P, G * H // LIST_ROWS], U16, name="list1")
+        list2 = keep.tile([P, G * N // LIST_ROWS], U16, name="list2")
+        w1_all = keep.tile([P, E * H], U32, name="w1_all", align_bytes=64)
+        s1_all = keep.tile([P, E * H], U8, name="s1_all", tag="shared", align_bytes=64)
+        s2_all = keep.tile([P, E * N], U8, name="s2_all", align_bytes=64)
+        x_codes = keep.tile([P, T], U32, name="x_codes", align_bytes=64)
+        x_plane = keep.tile([P, T], U8, name="x_plane", align_bytes=64)
+        gate_rows = keep.tile([P, P], F32, name="gate_rows", tag="early", align_bytes=64)
+        gate_cols = keep.tile([P, G * TILES], F32, name="gate_cols", align_bytes=64)
+        ident = keep.tile([P, P], F32, name="ident", align_bytes=64)
+        warm = keep.tile([P, 2], F32, name="warm", align_bytes=64)
+
+        nc.scalar.dma_start(out=w1_all[:].bitcast(I32), in_=words_of(w1_words))
+        nc.scalar.dma_start(out=x_codes[:].bitcast(I32), in_=words_of(x_words))
+        nc.sync.dma_start(list1[:], offs)
+        nc.sync.dma_start(list2[:], offs2)
+        nc.vector.memset(s1_all[:].bitcast(I32), 0)
+        nc.vector.memset(warm[:, 0:1], 0.0)
+        nc.vector.memset(s2_all[:].bitcast(I32), 0)
+        nc.scalar.activation(out=warm[:, 1:2], in_=warm[:, 0:1], func=SILU)
+        load_scales(nc.sync, s1_all, w1_scales, W1_ROW)
+        nc.gpsimd.memset(gate_rows[:], 0.0)
+        make_identity(nc, ident[:])
+        gate_runs = gate.rearrange("r p (m t) -> (r p m) t", t=P)
+        nc.gpsimd.dma_start(out=gate_rows[0 : G * TILES, :], in_=gate_runs[0 : G * P * TILES : P + 1, :])
+        load_scales(nc.gpsimd, x_plane, x_scales, X_ROW)
+        load_scales(nc.sync, s2_all, w2_scales, W2_ROW)
+
+        def gather(name, window, offsets, r, dtype, tag=""):
+            picked = keep.tile([P, H], dtype, name=f"{name}{r}", tag=tag or f"{name}{r}", align_bytes=64)
+            cols = H // LIST_ROWS
+            nc.vector.tensor_copy(picked[:], window[:].indirect(offsets[:, r * cols : (r + 1) * cols]))
+            return picked
+
+        s1 = [gather("s1_", s1_all, list1, r, U8) for r in range(G)]
+
+        gate_turned = psum.tile([P, 2 * TPC, P], F32, name="gate_turned", tag="turn", bufs=2)
+        nc.tensor.transpose(gate_turned[:, 0, :], gate_rows[:], ident[:])
+        nc.vector.tensor_copy(gate_cols[:], gate_turned[:, 0, 0 : G * TILES])
+
+        w2_all = keep.tile([P, E * N], U32, name="w2_all", tag="early", align_bytes=64)
+        nc.sync.dma_start(out=w2_all[:].bitcast(I32), in_=words_of(w2_words))
+
+        w1 = [gather("w1_", w1_all, list1, r, U32, "shared" if r == 0 else "") for r in range(G)]
+
+        units = [(c, r) for c in range(CHUNKS) for r in range(G)]
+        acts, gated, turned, grouped, codes, planes, w2, s2 = {}, {}, {}, {}, {}, {}, {}, {}
+
+        def first_product(u):
+            c, r = units[u]
+            for a in range(TPC):
+                cols = slice((c * TPC + a) * P, (c * TPC + a + 1) * P)
+                pre = psum.tile([P, H], F32, name="pre", tag="pre", bufs=3)
+                nc.tensor.matmul_mx(
+                    out=pre[:],
+                    lhsT=x_codes[:, cols].bitcast(FP8X4),
+                    lhsT_scale=x_plane[X_ROW:P, cols],
+                    rhs=w1[r][:].bitcast(FP8X4),
+                    rhs_scale=s1[r][W1_ROW:P, :],
+                    start=True,
+                    stop=True,
+                )
+                acts[u, a] = work.tile([P, H], F32, name="act", tag="act", bufs=8)
+                nc.scalar.activation(
+                    out=acts[u, a][:].rearrange("t (v p e) -> t v p e", v=2, e=2),
+                    in_=pre[:].rearrange("t (p v e) -> t v p e", v=2, e=2),
+                    func=SILU,
+                )
+
+        def gate_and_turn(u):
+            c, r = units[u]
+            turned[u] = psum.tile([P, 2 * TPC, P], F32, name="turned", tag="turn", bufs=2)
+            for a in range(TPC):
+                col = r * TILES + c * TPC + a
+                gated[u, a] = work.tile([P, H], BF16, name="gated", tag="gated", bufs=6, align_bytes=64)
+                nc.vector.tensor_scalar(gated[u, a][:], acts[u, a][:], gate_cols[:, col : col + 1], None, MULT)
+            for a in range(TPC):
+                pairs = gated[u, a][:].bitcast(F32)
+                for v in range(2):
+                    nc.tensor.transpose(turned[u][:, 2 * a + v, :], pairs[:, v * P : (v + 1) * P], ident[:])
+
+        def regroup(u, engine_copy):
+            grouped[u] = work.tile([P, CHUNK * PACK], BF16, name="grouped", tag="grouped", bufs=3, align_bytes=64)
+            engine_copy(
+                grouped[u][:].bitcast(F32).rearrange("p (a t v) -> p a t v", a=TPC, v=2),
+                turned[u][:].rearrange("p (a v) t -> p a t v", v=2),
+            )
+
+        def quantize(u):
+            codes[u] = work.tile([P, CHUNK], U32, name="codes", tag="codes", bufs=8, align_bytes=64)
+            planes[u] = work.tile([P, CHUNK], U8, name="planes", tag="planes", bufs=8, align_bytes=64)
+            nc.vector.quantize_mx(out=codes[u][:].bitcast(FP8X4), scales=planes[u][:], in_=grouped[u][:])
+
+        def second_product(c, copies):
+            for half in range(2):
+                acc = psum.tile([P, 2, CHUNK], F32, name="acc", tag="acc", bufs=3)
+                for j in range(2):
+                    cols = slice((2 * half + j) * P, (2 * half + j + 1) * P)
+                    for r in range(G):
+                        nc.tensor.matmul_mx(
+                            out=acc[:, j, :],
+                            lhsT=w2[r][:, cols].bitcast(FP8X4),
+                            lhsT_scale=s2[r][W2_ROW:P, cols],
+                            rhs=codes[G * c + r][:].bitcast(FP8X4),
+                            rhs_scale=planes[G * c + r][:],
+                            start=(r == 0),
+                            stop=(r == G - 1),
+                        )
+                result = work.tile([P, 2, CHUNK], F32, name="result", tag="result", bufs=4)
+                copies[half](result[:], acc[:])
+                rows = out[2 * half * P : 2 * (half + 1) * P, c * CHUNK : (c + 1) * CHUNK]
+                nc.sync.dma_start(out=rows.rearrange("(j p) t -> p j t", p=P), in_=result[:])
+
+        def multiply(acc, c, j, r):
+            cols = slice(j * P, (j + 1) * P)
+            nc.tensor.matmul_mx(
+                out=acc,
+                lhsT=w2[r][:, cols].bitcast(FP8X4),
+                lhsT_scale=s2[r][W2_ROW:P, cols],
+                rhs=codes[G * c + r][:].bitcast(FP8X4),
+                rhs_scale=planes[G * c + r][:],
+                start=(r == 0),
+                stop=(r == G - 1),
+            )
+
+        last = {}
+
+        def open_last():
+            for j in range(4):
+                last[j] = psum.tile([P, CHUNK], F32, name="last", tag="acc" if j == 3 else "pre", bufs=3)
+                multiply(last[j][:], CHUNKS - 1, j, 0)
+
+        def close_last():
+            for j in range(4):
+                multiply(last[j][:], CHUNKS - 1, j, 1)
+                result = work.tile([P, CHUNK], F32, name="tail", tag="tail", bufs=4)
+                (on_scalar, on_vector)[j % 2](result[:], last[j][:])
+                nc.sync.dma_start(out=out[j * P : (j + 1) * P, T - CHUNK : T], in_=result[:])
+
+        on_scalar, on_vector = nc.scalar.copy, nc.vector.tensor_copy
+        copies = ((on_vector, on_vector), (on_scalar, on_vector), (on_scalar, on_scalar))
+        steps = len(units)
+        for step in range(steps + 5):
+            if step < steps:
+                first_product(step)
+            if 0 <= step - 2 < steps:
+                gate_and_turn(step - 2)
+            if 0 <= step - 4 < steps:
+                quantize(step - 4)
+            if 0 <= step - 3 < steps:
+                regroup(step - 3, on_scalar)
+            if step in (2, 3):
+                s2[step - 2] = gather("s2_", s2_all, list2, step - 2, U8)
+            if step in (3, 4):
+                w2[step - 3] = gather("w2_", w2_all, list2, step - 3, U32)
+            if step - 4 == steps - 2:
+                open_last()
+            elif step - 4 == steps - 1:
+                close_last()
+            elif step - 4 >= 0 and (step - 4) % G == G - 1:
+                second_product((step - 4) // G, copies[(step - 4) // G])

@@ -74,90 +74,92 @@ def tile_moe_wsel_b_silu_p_kernel(
         load_scales(nc.gpsimd, x_plane, x_scales, X_ROW)
         load_scales(nc.sync, s2_all, w2_scales, W2_ROW)
 
-        def gather(name, window, offsets, r, dtype, tag=""):
-            picked = keep.tile([P, H], dtype, name=f"{name}{r}", tag=tag or f"{name}{r}", align_bytes=64)
+        def gather(picked, window, offsets, r):
             cols = H // LIST_ROWS
-            nc.vector.tensor_copy(picked[:], window[:].indirect(offsets[:, r * cols : (r + 1) * cols]))
-            return picked
+            nc.vector.tensor_copy(picked, window[:].indirect(offsets[:, r * cols : (r + 1) * cols]))
 
-        s1 = [gather("s1_", s1_all, list1, r, U8) for r in range(G)]
+        def bank(shape, name, number):
+            return psum.tile(shape, F32, name=name, tag=f"bank{number}")
 
-        gate_turned = psum.tile([P, 2 * TPC, P], F32, name="gate_turned", tag="turn", bufs=2)
-        nc.tensor.transpose(gate_turned[:, 0, :], gate_rows[:], ident[:])
-        nc.vector.tensor_copy(gate_cols[:], gate_turned[:, 0, 0 : G * TILES])
+        s1 = [keep.tile([P, H], U8, name=f"s1_{r}", align_bytes=64) for r in range(G)]
+        for r in range(G):
+            gather(s1[r][:], s1_all, list1, r)
 
+        gate_turned = bank([P, P], "gate_turned", 7)
+        nc.tensor.transpose(gate_turned[:], gate_rows[:], ident[:])
+        nc.vector.tensor_copy(gate_cols[:], gate_turned[:, 0 : G * TILES])
         w2_all = keep.tile([P, E * N], U32, name="w2_all", tag="early", align_bytes=64)
         nc.sync.dma_start(out=w2_all[:].bitcast(I32), in_=words_of(w2_words))
 
-        w1 = [gather("w1_", w1_all, list1, r, U32, "shared" if r == 0 else "") for r in range(G)]
+        w1 = keep.tile([P, G * H], U32, name="w1", tag="shared", align_bytes=64)
+        for r in range(G):
+            gather(w1[:, r * H : (r + 1) * H], w1_all, list1, r)
 
-        units = [(c, r) for c in range(CHUNKS) for r in range(G)]
-        acts, gated, turned, grouped, codes, planes, w2, s2 = {}, {}, {}, {}, {}, {}, {}, {}
+        acts, gated, turned, grouped, codes, planes, w2, s2, last, late = {}, {}, {}, {}, {}, {}, {}, {}, {}, {}
+        turn_banks = (6, 7, 4, 5, 0, 1, 2, 3)
+        acc_banks = ((6, 7), (4, 5), (0, 1))
+        last_banks = (6, 7, 4, 5)
+        copy = {"S": nc.scalar.copy, "V": nc.vector.tensor_copy}
+        on_gpsimd = ()
 
-        def first_product(u):
-            c, r = units[u]
-            for a in range(TPC):
-                cols = slice((c * TPC + a) * P, (c * TPC + a + 1) * P)
-                pre = psum.tile([P, H], F32, name="pre", tag="pre", bufs=3)
-                nc.tensor.matmul_mx(
-                    out=pre[:],
-                    lhsT=x_codes[:, cols].bitcast(FP8X4),
-                    lhsT_scale=x_plane[X_ROW:P, cols],
-                    rhs=w1[r][:].bitcast(FP8X4),
-                    rhs_scale=s1[r][W1_ROW:P, :],
-                    start=True,
-                    stop=True,
-                )
-                acts[u, a] = work.tile([P, H], F32, name="act", tag="act", bufs=8)
-                nc.scalar.activation(
-                    out=acts[u, a][:].rearrange("t (v p e) -> t v p e", v=2, e=2),
-                    in_=pre[:].rearrange("t (p v e) -> t v p e", v=2, e=2),
-                    func=SILU,
-                )
+        def place(k):
+            u, a = divmod(k, TPC)
+            c, r = divmod(u, G)
+            return r, c * TPC + a
 
-        def gate_and_turn(u):
-            c, r = units[u]
-            turned[u] = psum.tile([P, 2 * TPC, P], F32, name="turned", tag="turn", bufs=2)
+        def first_product(k):
+            r, m = place(k)
+            cols = slice(m * P, (m + 1) * P)
+            pre = bank([P, H], "pre", k % 6)
+            nc.tensor.matmul_mx(
+                out=pre[:],
+                lhsT=x_codes[:, cols].bitcast(FP8X4),
+                lhsT_scale=x_plane[X_ROW:P, cols],
+                rhs=w1[:, r * H : (r + 1) * H].bitcast(FP8X4),
+                rhs_scale=s1[r][W1_ROW:P, :],
+                start=True,
+                stop=True,
+            )
+            acts[k] = work.tile([P, H], F32, name="act", tag=f"act{k}", align_bytes=64)
+            nc.scalar.activation(
+                out=acts[k][:].rearrange("t (v p e) -> t v p e", v=2, e=2),
+                in_=pre[:].rearrange("t (p v e) -> t v p e", v=2, e=2),
+                func=SILU,
+            )
+
+        def apply_gate(k):
+            r, m = place(k)
+            col = r * TILES + m
+            if k == 4:
+                late[0] = keep.tile([P, 12 * H], BF16, name="late", tag="early", align_bytes=64)
+            if k < 4 or k in on_gpsimd:
+                own = work.tile([P, H], BF16, name="gated", tag=f"gated{k}", align_bytes=64)
+                gated[k] = own[:]
+            else:
+                gated[k] = late[0][:, (k - 4) * H : (k - 3) * H]
+            if k in on_gpsimd:
+                nc.gpsimd.tensor_scalar(gated[k], acts[k][:], gate_cols[:, col : col + 1], 0.0, MULT, mybir.AluOpType.add)
+            else:
+                nc.vector.tensor_scalar(gated[k], acts[k][:], gate_cols[:, col : col + 1], None, MULT)
+
+        def turn(u):
+            turned[u] = bank([P, 2 * TPC, P], "turned", turn_banks[u])
             for a in range(TPC):
-                col = r * TILES + c * TPC + a
-                gated[u, a] = work.tile([P, H], BF16, name="gated", tag="gated", bufs=6, align_bytes=64)
-                nc.vector.tensor_scalar(gated[u, a][:], acts[u, a][:], gate_cols[:, col : col + 1], None, MULT)
-            for a in range(TPC):
-                pairs = gated[u, a][:].bitcast(F32)
+                pairs = gated[TPC * u + a].bitcast(F32)
                 for v in range(2):
                     nc.tensor.transpose(turned[u][:, 2 * a + v, :], pairs[:, v * P : (v + 1) * P], ident[:])
 
-        def regroup(u, engine_copy):
-            grouped[u] = work.tile([P, CHUNK * PACK], BF16, name="grouped", tag="grouped", bufs=3, align_bytes=64)
-            engine_copy(
+        def regroup(u, engine):
+            grouped[u] = work.tile([P, CHUNK * PACK], BF16, name="grouped", tag=f"grouped{u}", align_bytes=64)
+            copy[engine](
                 grouped[u][:].bitcast(F32).rearrange("p (a t v) -> p a t v", a=TPC, v=2),
                 turned[u][:].rearrange("p (a v) t -> p a t v", v=2),
             )
 
         def quantize(u):
-            codes[u] = work.tile([P, CHUNK], U32, name="codes", tag="codes", bufs=8, align_bytes=64)
-            planes[u] = work.tile([P, CHUNK], U8, name="planes", tag="planes", bufs=8, align_bytes=64)
+            codes[u] = work.tile([P, CHUNK], U32, name="codes", tag=f"codes{u}", align_bytes=64)
+            planes[u] = work.tile([P, CHUNK], U8, name="planes", tag=f"planes{u}", align_bytes=64)
             nc.vector.quantize_mx(out=codes[u][:].bitcast(FP8X4), scales=planes[u][:], in_=grouped[u][:])
-
-        def second_product(c, copies):
-            for half in range(2):
-                acc = psum.tile([P, 2, CHUNK], F32, name="acc", tag="acc", bufs=3)
-                for j in range(2):
-                    cols = slice((2 * half + j) * P, (2 * half + j + 1) * P)
-                    for r in range(G):
-                        nc.tensor.matmul_mx(
-                            out=acc[:, j, :],
-                            lhsT=w2[r][:, cols].bitcast(FP8X4),
-                            lhsT_scale=s2[r][W2_ROW:P, cols],
-                            rhs=codes[G * c + r][:].bitcast(FP8X4),
-                            rhs_scale=planes[G * c + r][:],
-                            start=(r == 0),
-                            stop=(r == G - 1),
-                        )
-                result = work.tile([P, 2, CHUNK], F32, name="result", tag="result", bufs=4)
-                copies[half](result[:], acc[:])
-                rows = out[2 * half * P : 2 * (half + 1) * P, c * CHUNK : (c + 1) * CHUNK]
-                nc.sync.dma_start(out=rows.rearrange("(j p) t -> p j t", p=P), in_=result[:])
 
         def multiply(acc, c, j, r):
             cols = slice(j * P, (j + 1) * P)
@@ -171,39 +173,45 @@ def tile_moe_wsel_b_silu_p_kernel(
                 stop=(r == G - 1),
             )
 
-        last = {}
+        def second_product(c, half, engine):
+            acc = bank([P, 2, CHUNK], "acc", acc_banks[c][half])
+            for j in range(2):
+                for r in range(G):
+                    multiply(acc[:, j, :], c, 2 * half + j, r)
+            result = work.tile([P, 2, CHUNK], F32, name="result", tag="result", bufs=4)
+            copy[engine](result[:], acc[:])
+            rows = out[2 * half * P : 2 * (half + 1) * P, c * CHUNK : (c + 1) * CHUNK]
+            nc.sync.dma_start(out=rows.rearrange("(j p) t -> p j t", p=P), in_=result[:])
 
-        def open_last():
-            for j in range(4):
-                last[j] = psum.tile([P, CHUNK], F32, name="last", tag="acc" if j == 3 else "pre", bufs=3)
-                multiply(last[j][:], CHUNKS - 1, j, 0)
-
-        def close_last():
-            for j in range(4):
-                multiply(last[j][:], CHUNKS - 1, j, 1)
-                result = work.tile([P, CHUNK], F32, name="tail", tag="tail", bufs=4)
-                (on_scalar, on_vector)[j % 2](result[:], last[j][:])
-                nc.sync.dma_start(out=out[j * P : (j + 1) * P, T - CHUNK : T], in_=result[:])
-
-        on_scalar, on_vector = nc.scalar.copy, nc.vector.tensor_copy
-        copies = ((on_vector, on_vector), (on_scalar, on_vector), (on_scalar, on_scalar))
-        steps = len(units)
-        for step in range(steps + 5):
-            if step < steps:
-                first_product(step)
-            if 0 <= step - 2 < steps:
-                gate_and_turn(step - 2)
-            if 0 <= step - 4 < steps:
-                quantize(step - 4)
-            if 0 <= step - 3 < steps:
-                regroup(step - 3, on_scalar)
-            if step in (2, 3):
-                s2[step - 2] = gather("s2_", s2_all, list2, step - 2, U8)
-            if step in (3, 4):
-                w2[step - 3] = gather("w2_", w2_all, list2, step - 3, U32)
-            if step - 4 == steps - 2:
-                open_last()
-            elif step - 4 == steps - 1:
-                close_last()
-            elif step - 4 >= 0 and (step - 4) % G == G - 1:
-                second_product((step - 4) // G, copies[(step - 4) // G])
+        for token in "F0 F1 F2 F3 F4 F5 G0 G1 T0 gs2_0 G2 G3 T1 gs2_1 R0S R1S Q0 Q1 gw2_0 gw2_1 F6 F7 F8 F9 F10 F11 F12 F13 M00S M01S G4 G5 T2 G6 G7 T3 R2S R3S Q2 Q3 F14 F15 M10V M11S G8 G9 T4 G10 G11 T5 R4S R5S Q4 Q5 G12 G13 T6 G14 G15 T7 R6V R7S M20S M21S Q6 O Q7 CSVSV".split():
+            kind, rest = token[0], token[1:]
+            if kind == "F":
+                first_product(int(rest))
+            elif kind == "G":
+                apply_gate(int(rest))
+            elif kind == "T":
+                turn(int(rest))
+            elif kind == "R":
+                regroup(int(rest[0]), rest[1])
+            elif kind == "Q":
+                quantize(int(rest))
+            elif kind == "g" and rest[0] == "s":
+                r = int(rest[-1])
+                s2[r] = work.tile([P, N], U8, name="s2", tag=f"act{2 * r + 1}", align_bytes=64)
+                gather(s2[r][:], s2_all, list2, r)
+            elif kind == "g":
+                r = int(rest[-1])
+                w2[r] = work.tile([P, N], U32, name="w2", tag=f"grouped{r}", align_bytes=64)
+                gather(w2[r][:], w2_all, list2, r)
+            elif kind == "M":
+                second_product(int(rest[0]), int(rest[1]), rest[2])
+            elif kind == "O":
+                for j in range(4):
+                    last[j] = bank([P, CHUNK], "last", last_banks[j])
+                    multiply(last[j][:], CHUNKS - 1, j, 0)
+            else:
+                for j in range(4):
+                    multiply(last[j][:], CHUNKS - 1, j, 1)
+                    result = work.tile([P, CHUNK], F32, name="tail", tag="tail", bufs=4)
+                    copy[rest[j]](result[:], last[j][:])
+                    nc.sync.dma_start(out=out[j * P : (j + 1) * P, T - CHUNK : T], in_=result[:])

@@ -48,30 +48,33 @@ def tile_moe_wsel_b_silu_p_kernel(
 
         list1 = keep.tile([P, G * H // LIST_ROWS], U16, name="list1")
         list2 = keep.tile([P, G * N // LIST_ROWS], U16, name="list2")
-        w1_all = keep.tile([P, E * H], U32, name="w1_all", align_bytes=64)
-        s1_all = keep.tile([P, E * H], U8, name="s1_all", tag="shared", align_bytes=64)
+        zeros = keep.tile([P, P], F32, name="zeros", tag="first", align_bytes=64)
+        s1_all = keep.tile([P, E * H], U8, name="s1_all", align_bytes=64)
         s2_all = keep.tile([P, E * N], U8, name="s2_all", align_bytes=64)
         x_codes = keep.tile([P, T], U32, name="x_codes", align_bytes=64)
         x_plane = keep.tile([P, T], U8, name="x_plane", align_bytes=64)
-        gate_rows = keep.tile([P, P], F32, name="gate_rows", tag="early", align_bytes=64)
+        gate_rows = keep.tile([P, P], F32, name="gate_rows", tag="shared", align_bytes=64)
         gate_cols = keep.tile([P, G * TILES], F32, name="gate_cols", align_bytes=64)
         ident = keep.tile([P, P], F32, name="ident", align_bytes=64)
         warm = keep.tile([P, 2], F32, name="warm", align_bytes=64)
 
-        nc.scalar.dma_start(out=w1_all[:].bitcast(I32), in_=words_of(w1_words))
         nc.scalar.dma_start(out=x_codes[:].bitcast(I32), in_=words_of(x_words))
         nc.sync.dma_start(list1[:], offs)
         nc.sync.dma_start(list2[:], offs2)
+        nc.vector.memset(zeros[:], 0.0)
         nc.vector.memset(s1_all[:].bitcast(I32), 0)
+        make_identity(nc, ident[:])
+        nc.vector.tensor_copy(gate_rows[:], zeros[:])
         nc.vector.memset(warm[:, 0:1], 0.0)
+        nc.vector.memset(x_plane[:].bitcast(I32), 0)
         nc.vector.memset(s2_all[:].bitcast(I32), 0)
         nc.scalar.activation(out=warm[:, 1:2], in_=warm[:, 0:1], func=SILU)
         load_scales(nc.sync, s1_all, w1_scales, W1_ROW)
-        nc.gpsimd.memset(gate_rows[:], 0.0)
-        make_identity(nc, ident[:])
+        w1_all = keep.tile([P, E * H], U32, name="w1_all", tag="first", align_bytes=64)
+        nc.sync.dma_start(out=w1_all[:].bitcast(I32), in_=words_of(w1_words))
         gate_runs = gate.rearrange("r p (m t) -> (r p m) t", t=P)
-        nc.gpsimd.dma_start(out=gate_rows[0 : G * TILES, :], in_=gate_runs[0 : G * P * TILES : P + 1, :])
-        load_scales(nc.gpsimd, x_plane, x_scales, X_ROW)
+        nc.sync.dma_start(out=gate_rows[0 : G * TILES, :], in_=gate_runs[0 : G * P * TILES : P + 1, :])
+        load_scales(nc.sync, x_plane, x_scales, X_ROW)
         load_scales(nc.sync, s2_all, w2_scales, W2_ROW)
 
         def gather(picked, window, offsets, r):
@@ -87,11 +90,11 @@ def tile_moe_wsel_b_silu_p_kernel(
 
         gate_turned = bank([P, P], "gate_turned", 7)
         nc.tensor.transpose(gate_turned[:], gate_rows[:], ident[:])
-        nc.vector.tensor_copy(gate_cols[:], gate_turned[:, 0 : G * TILES])
-        w2_all = keep.tile([P, E * N], U32, name="w2_all", tag="early", align_bytes=64)
-        nc.sync.dma_start(out=w2_all[:].bitcast(I32), in_=words_of(w2_words))
+        nc.scalar.copy(gate_cols[:], gate_turned[:, 0 : G * TILES])
+        w2_all = keep.tile([P, E * N], U32, name="w2_all", tag="shared", align_bytes=64)
+        nc.scalar.dma_start(out=w2_all[:].bitcast(I32), in_=words_of(w2_words))
 
-        w1 = keep.tile([P, G * H], U32, name="w1", tag="shared", align_bytes=64)
+        w1 = keep.tile([P, G * H], U32, name="w1", align_bytes=64)
         for r in range(G):
             gather(w1[:, r * H : (r + 1) * H], w1_all, list1, r)
 
@@ -131,7 +134,7 @@ def tile_moe_wsel_b_silu_p_kernel(
             r, m = place(k)
             col = r * TILES + m
             if k == 4:
-                late[0] = keep.tile([P, 12 * H], BF16, name="late", tag="early", align_bytes=64)
+                late[0] = keep.tile([P, 12 * H], BF16, name="late", tag="shared", align_bytes=64)
             if k < 4 or k in on_gpsimd:
                 own = work.tile([P, H], BF16, name="gated", tag=f"gated{k}", align_bytes=64)
                 gated[k] = own[:]
@@ -183,7 +186,7 @@ def tile_moe_wsel_b_silu_p_kernel(
             rows = out[2 * half * P : 2 * (half + 1) * P, c * CHUNK : (c + 1) * CHUNK]
             nc.sync.dma_start(out=rows.rearrange("(j p) t -> p j t", p=P), in_=result[:])
 
-        for token in "F0 F1 F2 F3 F4 F5 G0 G1 T0 gs2_0 G2 G3 T1 gs2_1 R0S R1S Q0 Q1 gw2_0 gw2_1 F6 F7 F8 F9 F10 F11 F12 F13 M00S M01S G4 G5 T2 G6 G7 T3 R2S R3S Q2 Q3 F14 F15 M10V M11S G8 G9 T4 G10 G11 T5 R4S R5S Q4 Q5 G12 G13 T6 G14 G15 T7 R6V R7S M20S M21S Q6 O Q7 CSVSV".split():
+        for token in "F0 F1 F2 F3 F4 F5 G0 G1 T0 gs2_0 G2 G3 T1 gs2_1 R0S R1S Q0 Q1 gw2_0 gw2_1 F6 F7 F8 F9 F10 F11 F12 F13 M00S M01S G4 G5 T2 G6 G7 T3 R2S R3S Q2 Q3 F14 F15 M10V M11S G8 G9 T4 G10 G11 T5 R4S R5S Q4 Q5 G12 G13 T6 G14 G15 T7 R6S R7S M20V M21S Q6 O Q7 CSVSV".split():
             kind, rest = token[0], token[1:]
             if kind == "F":
                 first_product(int(rest))
@@ -197,11 +200,11 @@ def tile_moe_wsel_b_silu_p_kernel(
                 quantize(int(rest))
             elif kind == "g" and rest[0] == "s":
                 r = int(rest[-1])
-                s2[r] = work.tile([P, N], U8, name="s2", tag=f"act{2 * r + 1}", align_bytes=64)
+                s2[r] = work.tile([P, N], U8, name="s2", tag=("act0", "act2")[r], align_bytes=64)
                 gather(s2[r][:], s2_all, list2, r)
             elif kind == "g":
                 r = int(rest[-1])
-                w2[r] = work.tile([P, N], U32, name="w2", tag=f"grouped{r}", align_bytes=64)
+                w2[r] = work.tile([P, N], U32, name="w2", tag=("act3", "grouped1")[r], align_bytes=64)
                 gather(w2[r][:], w2_all, list2, r)
             elif kind == "M":
                 second_product(int(rest[0]), int(rest[1]), rest[2])

@@ -4,8 +4,9 @@ import concourse.mybir as mybir
 from concourse.masks import make_identity
 
 K, T, E, G, H, N = 512, 1024, 8, 2, 512, 512
+P = 128
 FLOPS = 2 * T * G * (K * H + H * N)
-BYTES = K * T + K * E * H + H * E * N + (K // 32) * (T + E * H + E * N) + 4 * G * T + 2 * 2 * 128 * 64 + 4 * N * T
+BYTES = (K + K // 32) * (T + E * H + E * N) + 4 * G * T + 2 * P * G * (H + N) // 16 + 4 * N * T
 
 F32 = mybir.dt.float32
 BF16 = mybir.dt.bfloat16
@@ -14,17 +15,18 @@ U32 = mybir.dt.uint32
 U16 = mybir.dt.uint16
 U8 = mybir.dt.uint8
 FP8X4 = mybir.dt.float8_e4m3fn_x4
-SILU = mybir.ActivationFunctionType.Silu
-MULT = mybir.AluOpType.mult
 
-P = 128
 PACK = 4
 LIST_ROWS = 16
 TILES = T // P
-CHUNK = 256
+PAIR = 2
+CHUNK = PAIR * P
 CHUNKS = T // CHUNK
-TPC = CHUNK // P
+UNITS = CHUNKS * G
+ROW_BLOCKS = N // P
 W1_ROW, X_ROW, W2_ROW = 4, 8, 12
+RING_BANKS, TURN_BANK, SUM_BANK = 4, 4, 6
+VECTOR_EVERY = 3
 
 
 def load_scales(queue, plane, scales, row):
@@ -46,17 +48,22 @@ def tile_moe_wsel_b_silu_p_kernel(
         work = ctx.enter_context(tc.tile_pool(name="work", bufs=1))
         psum = ctx.enter_context(tc.psum_pool(name="psum", bufs=1))
 
+        def bank(shape, name, number):
+            return psum.tile(shape, F32, name=name, tag=f"bank{number}")
+
+        def gather(picked, window, offsets, r):
+            cols = H // LIST_ROWS
+            nc.vector.tensor_copy(picked[:], window[:].indirect(offsets[:, r * cols : (r + 1) * cols]))
+
         list1 = keep.tile([P, G * H // LIST_ROWS], U16, name="list1")
         list2 = keep.tile([P, G * N // LIST_ROWS], U16, name="list2")
-        zeros = keep.tile([P, P], F32, name="zeros", tag="first", align_bytes=64)
-        s1_all = keep.tile([P, E * H], U8, name="s1_all", align_bytes=64)
+        zeros = keep.tile([P, P], F32, name="zeros", tag="w1_bytes", align_bytes=64)
+        s1_all = keep.tile([P, E * H], U8, name="s1_all", tag="w2_bytes", align_bytes=64)
         s2_all = keep.tile([P, E * N], U8, name="s2_all", align_bytes=64)
         x_codes = keep.tile([P, T], U32, name="x_codes", align_bytes=64)
         x_plane = keep.tile([P, T], U8, name="x_plane", align_bytes=64)
-        gate_rows = keep.tile([P, P], F32, name="gate_rows", tag="shared", align_bytes=64)
-        gate_cols = keep.tile([P, G * TILES], F32, name="gate_cols", align_bytes=64)
+        gate_rows = keep.tile([P, P], F32, name="gate_rows", align_bytes=64)
         ident = keep.tile([P, P], F32, name="ident", align_bytes=64)
-        warm = keep.tile([P, 2], F32, name="warm", align_bytes=64)
 
         nc.scalar.dma_start(out=x_codes[:].bitcast(I32), in_=words_of(x_words))
         nc.sync.dma_start(list1[:], offs)
@@ -65,156 +72,131 @@ def tile_moe_wsel_b_silu_p_kernel(
         nc.vector.memset(s1_all[:].bitcast(I32), 0)
         make_identity(nc, ident[:])
         nc.vector.tensor_copy(gate_rows[:], zeros[:])
-        nc.vector.memset(warm[:, 0:1], 0.0)
         nc.vector.memset(x_plane[:].bitcast(I32), 0)
         nc.vector.memset(s2_all[:].bitcast(I32), 0)
-        nc.scalar.activation(out=warm[:, 1:2], in_=warm[:, 0:1], func=SILU)
+
         load_scales(nc.sync, s1_all, w1_scales, W1_ROW)
-        w1_all = keep.tile([P, E * H], U32, name="w1_all", tag="first", align_bytes=64)
+        w1_all = keep.tile([P, E * H], U32, name="w1_all", tag="w1_bytes", align_bytes=64)
         nc.sync.dma_start(out=w1_all[:].bitcast(I32), in_=words_of(w1_words))
         gate_runs = gate.rearrange("r p (m t) -> (r p m) t", t=P)
         nc.sync.dma_start(out=gate_rows[0 : G * TILES, :], in_=gate_runs[0 : G * P * TILES : P + 1, :])
         load_scales(nc.sync, x_plane, x_scales, X_ROW)
-        load_scales(nc.sync, s2_all, w2_scales, W2_ROW)
-
-        def gather(picked, window, offsets, r):
-            cols = H // LIST_ROWS
-            nc.vector.tensor_copy(picked, window[:].indirect(offsets[:, r * cols : (r + 1) * cols]))
-
-        def bank(shape, name, number):
-            return psum.tile(shape, F32, name=name, tag=f"bank{number}")
+        load_scales(nc.gpsimd, s2_all, w2_scales, W2_ROW)
 
         s1 = [keep.tile([P, H], U8, name=f"s1_{r}", align_bytes=64) for r in range(G)]
         for r in range(G):
-            gather(s1[r][:], s1_all, list1, r)
-
-        gate_turned = bank([P, P], "gate_turned", 7)
-        nc.tensor.transpose(gate_turned[:], gate_rows[:], ident[:])
-        nc.scalar.copy(gate_cols[:], gate_turned[:, 0 : G * TILES])
-        w2_all = keep.tile([P, E * N], U32, name="w2_all", tag="shared", align_bytes=64)
-        nc.scalar.dma_start(out=w2_all[:].bitcast(I32), in_=words_of(w2_words))
-
-        w1 = keep.tile([P, G * H], U32, name="w1", align_bytes=64)
+            gather(s1[r], s1_all, list1, r)
+        w2_all = keep.tile([P, E * N], U32, name="w2_all", tag="w2_bytes", align_bytes=64)
+        nc.sync.dma_start(out=w2_all[:].bitcast(I32), in_=words_of(w2_words))
+        w1 = [keep.tile([P, H], U32, name=f"w1_{r}", align_bytes=64) for r in range(G)]
         for r in range(G):
-            gather(w1[:, r * H : (r + 1) * H], w1_all, list1, r)
+            gather(w1[r], w1_all, list1, r)
 
-        acts, gated, turned, grouped, codes, planes, w2, s2, last, late = {}, {}, {}, {}, {}, {}, {}, {}, {}, {}
-        turn_banks = (6, 7, 4, 5, 0, 1, 2, 3)
-        acc_banks = ((6, 7), (4, 5), (0, 1))
-        last_banks = (6, 7, 4, 5)
-        copy = {"S": nc.scalar.copy, "V": nc.vector.tensor_copy}
-        on_gpsimd = ()
+        gate_turned = bank([P, P], "gate_turned", SUM_BANK + 1)
+        nc.tensor.transpose(gate_turned[:], gate_rows[:], ident[:])
+        gate_cols = keep.tile([P, G * TILES], F32, name="gate_cols", tag="w1_bytes", align_bytes=64)
+        nc.vector.tensor_copy(gate_cols[:], gate_turned[:, 0 : G * TILES])
 
-        def place(k):
-            u, a = divmod(k, TPC)
+        acts, turned, grouped, codes, planes, s2, w2 = {}, {}, {}, {}, {}, {}, {}
+
+        def activate(u):
             c, r = divmod(u, G)
-            return r, c * TPC + a
+            for a in range(PAIR):
+                tokens = slice((c * PAIR + a) * P, (c * PAIR + a + 1) * P)
+                first = bank([P, H], "first", (u * PAIR + a) % RING_BANKS)
+                nc.tensor.matmul_mx(
+                    out=first[:],
+                    lhsT=x_codes[:, tokens].bitcast(FP8X4),
+                    lhsT_scale=x_plane[X_ROW:P, tokens],
+                    rhs=w1[r][:].bitcast(FP8X4),
+                    rhs_scale=s1[r][W1_ROW:P, :],
+                    start=True,
+                    stop=True,
+                )
+                acts[u, a] = work.tile([P, H], F32, name="act", tag=f"act{u}_{a}", align_bytes=64)
+                nc.scalar.activation(
+                    out=acts[u, a][:].rearrange("t (v p e) -> t v p e", v=2, e=2),
+                    in_=first[:].rearrange("t (p v e) -> t v p e", v=2, e=2),
+                    func=mybir.ActivationFunctionType.Silu,
+                )
 
-        def first_product(k):
-            r, m = place(k)
-            cols = slice(m * P, (m + 1) * P)
-            pre = bank([P, H], "pre", k % 6)
-            nc.tensor.matmul_mx(
-                out=pre[:],
-                lhsT=x_codes[:, cols].bitcast(FP8X4),
-                lhsT_scale=x_plane[X_ROW:P, cols],
-                rhs=w1[:, r * H : (r + 1) * H].bitcast(FP8X4),
-                rhs_scale=s1[r][W1_ROW:P, :],
-                start=True,
-                stop=True,
-            )
-            acts[k] = work.tile([P, H], F32, name="act", tag=f"act{k}", align_bytes=64)
-            nc.scalar.activation(
-                out=acts[k][:].rearrange("t (v p e) -> t v p e", v=2, e=2),
-                in_=pre[:].rearrange("t (p v e) -> t v p e", v=2, e=2),
-                func=SILU,
-            )
-
-        def apply_gate(k):
-            r, m = place(k)
-            col = r * TILES + m
-            if k == 4:
-                late[0] = keep.tile([P, 12 * H], BF16, name="late", tag="shared", align_bytes=64)
-            if k < 4 or k in on_gpsimd:
-                own = work.tile([P, H], BF16, name="gated", tag=f"gated{k}", align_bytes=64)
-                gated[k] = own[:]
-            else:
-                gated[k] = late[0][:, (k - 4) * H : (k - 3) * H]
-            if k in on_gpsimd:
-                nc.gpsimd.tensor_scalar(gated[k], acts[k][:], gate_cols[:, col : col + 1], 0.0, MULT, mybir.AluOpType.add)
-            else:
-                nc.vector.tensor_scalar(gated[k], acts[k][:], gate_cols[:, col : col + 1], None, MULT)
-
-        def turn(u):
-            turned[u] = bank([P, 2 * TPC, P], "turned", turn_banks[u])
-            for a in range(TPC):
-                pairs = gated[TPC * u + a].bitcast(F32)
+        def gate_and_turn(u):
+            c, r = divmod(u, G)
+            gated = work.tile([P, PAIR, H], BF16, name="gated", tag=f"gated{u}", align_bytes=64)
+            for a in range(PAIR):
+                col = r * TILES + c * PAIR + a
+                nc.vector.tensor_scalar(
+                    gated[:, a, :], acts[u, a][:], gate_cols[:, col : col + 1], None, mybir.AluOpType.mult
+                )
+                if u < G and a == PAIR - 1:
+                    s2[u] = work.tile([P, N], U8, name="s2", tag=f"act{u}_{a}", align_bytes=64)
+                    gather(s2[u], s2_all, list2, u)
+            turned[u] = bank([P, PAIR, 2, P], "turned", TURN_BANK + u % 2)
+            for a in range(PAIR):
+                pairs = gated[:, a, :].bitcast(F32)
                 for v in range(2):
-                    nc.tensor.transpose(turned[u][:, 2 * a + v, :], pairs[:, v * P : (v + 1) * P], ident[:])
+                    nc.tensor.transpose(turned[u][:, a, v, :], pairs[:, v * P : (v + 1) * P], ident[:])
 
-        def regroup(u, engine):
+        def regroup(u):
+            copy = nc.vector.tensor_copy if u % VECTOR_EVERY == 0 or u == UNITS - 1 else nc.scalar.copy
             grouped[u] = work.tile([P, CHUNK * PACK], BF16, name="grouped", tag=f"grouped{u}", align_bytes=64)
-            copy[engine](
-                grouped[u][:].bitcast(F32).rearrange("p (a t v) -> p a t v", a=TPC, v=2),
-                turned[u][:].rearrange("p (a v) t -> p a t v", v=2),
+            copy(
+                grouped[u][:].bitcast(F32).rearrange("p (a t v) -> p a t v", a=PAIR, v=2),
+                turned[u][:].rearrange("p a v t -> p a t v"),
             )
 
         def quantize(u):
             codes[u] = work.tile([P, CHUNK], U32, name="codes", tag=f"codes{u}", align_bytes=64)
             planes[u] = work.tile([P, CHUNK], U8, name="planes", tag=f"planes{u}", align_bytes=64)
             nc.vector.quantize_mx(out=codes[u][:].bitcast(FP8X4), scales=planes[u][:], in_=grouped[u][:])
+            if u < G:
+                w2[u] = work.tile([P, N], U32, name="w2", tag=f"grouped{u}", align_bytes=64)
+                gather(w2[u], w2_all, list2, u)
 
-        def multiply(acc, c, j, r):
-            cols = slice(j * P, (j + 1) * P)
+        def second_pass(total, c, j, r):
+            rows = slice(j * P, (j + 1) * P)
             nc.tensor.matmul_mx(
-                out=acc,
-                lhsT=w2[r][:, cols].bitcast(FP8X4),
-                lhsT_scale=s2[r][W2_ROW:P, cols],
+                out=total,
+                lhsT=w2[r][:, rows].bitcast(FP8X4),
+                lhsT_scale=s2[r][W2_ROW:P, rows],
                 rhs=codes[G * c + r][:].bitcast(FP8X4),
                 rhs_scale=planes[G * c + r][:],
                 start=(r == 0),
                 stop=(r == G - 1),
             )
 
-        def second_product(c, half, engine):
-            acc = bank([P, 2, CHUNK], "acc", acc_banks[c][half])
-            for j in range(2):
-                for r in range(G):
-                    multiply(acc[:, j, :], c, 2 * half + j, r)
-            result = work.tile([P, 2, CHUNK], F32, name="result", tag="result", bufs=4)
-            copy[engine](result[:], acc[:])
-            rows = out[2 * half * P : 2 * (half + 1) * P, c * CHUNK : (c + 1) * CHUNK]
-            nc.sync.dma_start(out=rows.rearrange("(j p) t -> p j t", p=P), in_=result[:])
+        def finish_chunk(c):
+            for half in range(2):
+                total = bank([P, 2, CHUNK], "total", SUM_BANK + half)
+                for j in range(2):
+                    for r in range(G):
+                        second_pass(total[:, j, :], c, 2 * half + j, r)
+                result = work.tile([P, 2, CHUNK], F32, name="result", tag="result", bufs=4)
+                copy = nc.vector.tensor_copy if (2 * c + half) % VECTOR_EVERY == 1 else nc.scalar.copy
+                copy(result[:], total[:])
+                rows = out[2 * half * P : 2 * (half + 1) * P, c * CHUNK : (c + 1) * CHUNK]
+                nc.sync.dma_start(out=rows.rearrange("(j p) t -> p j t", p=P), in_=result[:])
 
-        for token in "F0 F1 F2 F3 F4 F5 G0 G1 T0 gs2_0 G2 G3 T1 gs2_1 R0S R1S Q0 Q1 gw2_0 gw2_1 F6 F7 F8 F9 F10 F11 F12 F13 M00S M01S G4 G5 T2 G6 G7 T3 R2S R3S Q2 Q3 F14 F15 M10V M11S G8 G9 T4 G10 G11 T5 R4S R5S Q4 Q5 G12 G13 T6 G14 G15 T7 R6S R7S M20V M21S Q6 O Q7 CSVSV".split():
-            kind, rest = token[0], token[1:]
-            if kind == "F":
-                first_product(int(rest))
-            elif kind == "G":
-                apply_gate(int(rest))
-            elif kind == "T":
-                turn(int(rest))
-            elif kind == "R":
-                regroup(int(rest[0]), rest[1])
-            elif kind == "Q":
-                quantize(int(rest))
-            elif kind == "g" and rest[0] == "s":
-                r = int(rest[-1])
-                s2[r] = work.tile([P, N], U8, name="s2", tag=("act0", "act2")[r], align_bytes=64)
-                gather(s2[r][:], s2_all, list2, r)
-            elif kind == "g":
-                r = int(rest[-1])
-                w2[r] = work.tile([P, N], U32, name="w2", tag=("act3", "grouped1")[r], align_bytes=64)
-                gather(w2[r][:], w2_all, list2, r)
-            elif kind == "M":
-                second_product(int(rest[0]), int(rest[1]), rest[2])
-            elif kind == "O":
-                for j in range(4):
-                    last[j] = bank([P, CHUNK], "last", last_banks[j])
-                    multiply(last[j][:], CHUNKS - 1, j, 0)
-            else:
-                for j in range(4):
-                    multiply(last[j][:], CHUNKS - 1, j, 1)
-                    result = work.tile([P, CHUNK], F32, name="tail", tag="tail", bufs=4)
-                    copy[rest[j]](result[:], last[j][:])
-                    nc.sync.dma_start(out=out[j * P : (j + 1) * P, T - CHUNK : T], in_=result[:])
+        for step in range(UNITS + 3):
+            if step < UNITS:
+                activate(step)
+            if 0 <= step - 1 < UNITS:
+                gate_and_turn(step - 1)
+            done = step - 3
+            if done >= 0:
+                quantize(done)
+            if 0 <= step - 2 < UNITS:
+                regroup(step - 2)
+            if 0 <= done < UNITS - G and done % G == G - 1:
+                finish_chunk(done // G)
+            if done == UNITS - G:
+                tails = [bank([P, CHUNK], "tail", j) for j in range(ROW_BLOCKS)]
+                for j in range(ROW_BLOCKS):
+                    second_pass(tails[j][:], CHUNKS - 1, j, 0)
+
+        for j in range(ROW_BLOCKS):
+            second_pass(tails[j][:], CHUNKS - 1, j, G - 1)
+            result = work.tile([P, CHUNK], F32, name="last_result", tag="last_result", bufs=ROW_BLOCKS)
+            copy = nc.vector.tensor_copy if j % 2 == 0 else nc.scalar.copy
+            copy(result[:], tails[j][:])
+            nc.sync.dma_start(out=out[j * P : (j + 1) * P, T - CHUNK : T], in_=result[:])

@@ -5,8 +5,10 @@ from concourse.masks import make_identity
 
 K, T, E, G, H, N = 512, 1024, 8, 2, 512, 512
 P = 128
+PACK = 4
+LIST_ROWS = 16
 FLOPS = 2 * T * G * (K * H + H * N)
-BYTES = (K + K // 32) * (T + E * H + E * N) + 4 * G * T + 2 * P * G * (H + N) // 16 + 4 * N * T
+BYTES = (K + K // 32) * (T + E * H + E * N) + 4 * G * T + 2 * P * G * (H + N) // LIST_ROWS + 4 * N * T
 
 F32 = mybir.dt.float32
 BF16 = mybir.dt.bfloat16
@@ -16,8 +18,6 @@ U16 = mybir.dt.uint16
 U8 = mybir.dt.uint8
 FP8X4 = mybir.dt.float8_e4m3fn_x4
 
-PACK = 4
-LIST_ROWS = 16
 TILES = T // P
 PAIR = 2
 CHUNK = PAIR * P
@@ -25,8 +25,9 @@ CHUNKS = T // CHUNK
 UNITS = CHUNKS * G
 ROW_BLOCKS = N // P
 W1_ROW, X_ROW, W2_ROW = 4, 8, 12
-RING_BANKS, TURN_BANK, SUM_BANK = 4, 4, 6
-VECTOR_EVERY = 3
+PRE_BANKS, TURN_BANKS, SUM_BANKS = 3, 2, 3
+GATE_LAG, REGROUP_LAG, QUANTIZE_LAG = 2, 3, 4
+ACT_BUFS, GATED_BUFS, GROUPED_BUFS, RESULT_BUFS = 4 * PAIR, 3 * PAIR, 3, 4
 
 
 def load_scales(queue, plane, scales, row):
@@ -48,64 +49,57 @@ def tile_moe_wsel_b_silu_p_kernel(
         work = ctx.enter_context(tc.tile_pool(name="work", bufs=1))
         psum = ctx.enter_context(tc.psum_pool(name="psum", bufs=1))
 
-        def bank(shape, name, number):
-            return psum.tile(shape, F32, name=name, tag=f"bank{number}")
-
-        def gather(picked, window, offsets, r):
-            cols = H // LIST_ROWS
-            nc.vector.tensor_copy(picked[:], window[:].indirect(offsets[:, r * cols : (r + 1) * cols]))
-
         list1 = keep.tile([P, G * H // LIST_ROWS], U16, name="list1")
         list2 = keep.tile([P, G * N // LIST_ROWS], U16, name="list2")
-        zeros = keep.tile([P, P], F32, name="zeros", tag="w1_bytes", align_bytes=64)
-        s1_all = keep.tile([P, E * H], U8, name="s1_all", tag="w2_bytes", align_bytes=64)
+        w1_all = keep.tile([P, E * H], U32, name="w1_all", align_bytes=64)
+        s1_all = keep.tile([P, E * H], U8, name="s1_all", tag="shared", align_bytes=64)
         s2_all = keep.tile([P, E * N], U8, name="s2_all", align_bytes=64)
         x_codes = keep.tile([P, T], U32, name="x_codes", align_bytes=64)
         x_plane = keep.tile([P, T], U8, name="x_plane", align_bytes=64)
-        gate_rows = keep.tile([P, P], F32, name="gate_rows", align_bytes=64)
+        gate_rows = keep.tile([P, P], F32, name="gate_rows", tag="early", align_bytes=64)
+        gate_cols = keep.tile([P, G * TILES], F32, name="gate_cols", align_bytes=64)
         ident = keep.tile([P, P], F32, name="ident", align_bytes=64)
 
+        nc.scalar.dma_start(out=w1_all[:].bitcast(I32), in_=words_of(w1_words))
         nc.scalar.dma_start(out=x_codes[:].bitcast(I32), in_=words_of(x_words))
         nc.sync.dma_start(list1[:], offs)
         nc.sync.dma_start(list2[:], offs2)
-        nc.vector.memset(zeros[:], 0.0)
         nc.vector.memset(s1_all[:].bitcast(I32), 0)
-        make_identity(nc, ident[:])
-        nc.vector.tensor_copy(gate_rows[:], zeros[:])
-        nc.vector.memset(x_plane[:].bitcast(I32), 0)
         nc.vector.memset(s2_all[:].bitcast(I32), 0)
-
         load_scales(nc.sync, s1_all, w1_scales, W1_ROW)
-        w1_all = keep.tile([P, E * H], U32, name="w1_all", tag="w1_bytes", align_bytes=64)
-        nc.sync.dma_start(out=w1_all[:].bitcast(I32), in_=words_of(w1_words))
+        nc.gpsimd.memset(gate_rows[:], 0.0)
+        make_identity(nc, ident[:])
         gate_runs = gate.rearrange("r p (m t) -> (r p m) t", t=P)
-        nc.sync.dma_start(out=gate_rows[0 : G * TILES, :], in_=gate_runs[0 : G * P * TILES : P + 1, :])
-        load_scales(nc.sync, x_plane, x_scales, X_ROW)
-        load_scales(nc.gpsimd, s2_all, w2_scales, W2_ROW)
+        nc.gpsimd.dma_start(out=gate_rows[0 : G * TILES, :], in_=gate_runs[0 : G * P * TILES : P + 1, :])
+        load_scales(nc.gpsimd, x_plane, x_scales, X_ROW)
+        load_scales(nc.sync, s2_all, w2_scales, W2_ROW)
 
-        s1 = [keep.tile([P, H], U8, name=f"s1_{r}", align_bytes=64) for r in range(G)]
-        for r in range(G):
-            gather(s1[r], s1_all, list1, r)
-        w2_all = keep.tile([P, E * N], U32, name="w2_all", tag="w2_bytes", align_bytes=64)
+        def gather(name, window, offsets, r, dtype, tag):
+            picked = keep.tile([P, H], dtype, name=name, tag=tag, align_bytes=64)
+            cols = H // LIST_ROWS
+            nc.vector.tensor_copy(picked[:], window[:].indirect(offsets[:, r * cols : (r + 1) * cols]))
+            return picked
+
+        s1 = [gather(f"s1_{r}", s1_all, list1, r, U8, f"s1_{r}") for r in range(G)]
+
+        gate_turned = psum.tile([P, 2 * PAIR, P], F32, name="gate_turned", tag="turn", bufs=TURN_BANKS)
+        nc.tensor.transpose(gate_turned[:, 0, :], gate_rows[:], ident[:])
+        nc.vector.tensor_copy(gate_cols[:], gate_turned[:, 0, 0 : G * TILES])
+
+        w2_all = keep.tile([P, E * N], U32, name="w2_all", tag="early", align_bytes=64)
         nc.sync.dma_start(out=w2_all[:].bitcast(I32), in_=words_of(w2_words))
-        w1 = [keep.tile([P, H], U32, name=f"w1_{r}", align_bytes=64) for r in range(G)]
-        for r in range(G):
-            gather(w1[r], w1_all, list1, r)
 
-        gate_turned = bank([P, P], "gate_turned", SUM_BANK + 1)
-        nc.tensor.transpose(gate_turned[:], gate_rows[:], ident[:])
-        gate_cols = keep.tile([P, G * TILES], F32, name="gate_cols", tag="w1_bytes", align_bytes=64)
-        nc.vector.tensor_copy(gate_cols[:], gate_turned[:, 0 : G * TILES])
+        w1 = [gather(f"w1_{r}", w1_all, list1, r, U32, "shared" if r == 0 else f"w1_{r}") for r in range(G)]
 
-        acts, turned, grouped, codes, planes, s2, w2 = {}, {}, {}, {}, {}, {}, {}
+        acts, turned, grouped, codes, planes, w2, s2, last = {}, {}, {}, {}, {}, {}, {}, {}
 
-        def activate(u):
+        def first_product(u):
             c, r = divmod(u, G)
             for a in range(PAIR):
                 tokens = slice((c * PAIR + a) * P, (c * PAIR + a + 1) * P)
-                first = bank([P, H], "first", (u * PAIR + a) % RING_BANKS)
+                pre = psum.tile([P, H], F32, name="pre", tag="pre", bufs=PRE_BANKS)
                 nc.tensor.matmul_mx(
-                    out=first[:],
+                    out=pre[:],
                     lhsT=x_codes[:, tokens].bitcast(FP8X4),
                     lhsT_scale=x_plane[X_ROW:P, tokens],
                     rhs=w1[r][:].bitcast(FP8X4),
@@ -113,50 +107,46 @@ def tile_moe_wsel_b_silu_p_kernel(
                     start=True,
                     stop=True,
                 )
-                acts[u, a] = work.tile([P, H], F32, name="act", tag=f"act{u}_{a}", align_bytes=64)
+                acts[u, a] = work.tile([P, H], F32, name="act", tag="act", bufs=ACT_BUFS)
                 nc.scalar.activation(
                     out=acts[u, a][:].rearrange("t (v p e) -> t v p e", v=2, e=2),
-                    in_=first[:].rearrange("t (p v e) -> t v p e", v=2, e=2),
+                    in_=pre[:].rearrange("t (p v e) -> t v p e", v=2, e=2),
                     func=mybir.ActivationFunctionType.Silu,
                 )
 
         def gate_and_turn(u):
             c, r = divmod(u, G)
-            gated = work.tile([P, PAIR, H], BF16, name="gated", tag=f"gated{u}", align_bytes=64)
+            turned[u] = psum.tile([P, 2 * PAIR, P], F32, name="turned", tag="turn", bufs=TURN_BANKS)
+            gated = []
             for a in range(PAIR):
                 col = r * TILES + c * PAIR + a
+                gated.append(work.tile([P, H], BF16, name="gated", tag="gated", bufs=GATED_BUFS, align_bytes=64))
                 nc.vector.tensor_scalar(
-                    gated[:, a, :], acts[u, a][:], gate_cols[:, col : col + 1], None, mybir.AluOpType.mult
+                    gated[a][:], acts[u, a][:], gate_cols[:, col : col + 1], None, mybir.AluOpType.mult
                 )
-                if u < G and a == PAIR - 1:
-                    s2[u] = work.tile([P, N], U8, name="s2", tag=f"act{u}_{a}", align_bytes=64)
-                    gather(s2[u], s2_all, list2, u)
-            turned[u] = bank([P, PAIR, 2, P], "turned", TURN_BANK + u % 2)
             for a in range(PAIR):
-                pairs = gated[:, a, :].bitcast(F32)
+                pairs = gated[a][:].bitcast(F32)
                 for v in range(2):
-                    nc.tensor.transpose(turned[u][:, a, v, :], pairs[:, v * P : (v + 1) * P], ident[:])
+                    nc.tensor.transpose(turned[u][:, 2 * a + v, :], pairs[:, v * P : (v + 1) * P], ident[:])
 
         def regroup(u):
-            copy = nc.vector.tensor_copy if u % VECTOR_EVERY == 0 or u == UNITS - 1 else nc.scalar.copy
-            grouped[u] = work.tile([P, CHUNK * PACK], BF16, name="grouped", tag=f"grouped{u}", align_bytes=64)
-            copy(
+            grouped[u] = work.tile(
+                [P, CHUNK * PACK], BF16, name="grouped", tag="grouped", bufs=GROUPED_BUFS, align_bytes=64
+            )
+            nc.scalar.copy(
                 grouped[u][:].bitcast(F32).rearrange("p (a t v) -> p a t v", a=PAIR, v=2),
-                turned[u][:].rearrange("p a v t -> p a t v"),
+                turned[u][:].rearrange("p (a v) t -> p a t v", v=2),
             )
 
         def quantize(u):
-            codes[u] = work.tile([P, CHUNK], U32, name="codes", tag=f"codes{u}", align_bytes=64)
-            planes[u] = work.tile([P, CHUNK], U8, name="planes", tag=f"planes{u}", align_bytes=64)
+            codes[u] = work.tile([P, CHUNK], U32, name="codes", tag="codes", bufs=UNITS, align_bytes=64)
+            planes[u] = work.tile([P, CHUNK], U8, name="planes", tag="planes", bufs=UNITS, align_bytes=64)
             nc.vector.quantize_mx(out=codes[u][:].bitcast(FP8X4), scales=planes[u][:], in_=grouped[u][:])
-            if u < G:
-                w2[u] = work.tile([P, N], U32, name="w2", tag=f"grouped{u}", align_bytes=64)
-                gather(w2[u], w2_all, list2, u)
 
-        def second_pass(total, c, j, r):
+        def second_pass(acc, c, j, r):
             rows = slice(j * P, (j + 1) * P)
             nc.tensor.matmul_mx(
-                out=total,
+                out=acc,
                 lhsT=w2[r][:, rows].bitcast(FP8X4),
                 lhsT_scale=s2[r][W2_ROW:P, rows],
                 rhs=codes[G * c + r][:].bitcast(FP8X4),
@@ -165,38 +155,53 @@ def tile_moe_wsel_b_silu_p_kernel(
                 stop=(r == G - 1),
             )
 
-        def finish_chunk(c):
+        def second_product(c):
             for half in range(2):
-                total = bank([P, 2, CHUNK], "total", SUM_BANK + half)
+                acc = psum.tile([P, 2, CHUNK], F32, name="acc", tag="acc", bufs=SUM_BANKS)
                 for j in range(2):
                     for r in range(G):
-                        second_pass(total[:, j, :], c, 2 * half + j, r)
-                result = work.tile([P, 2, CHUNK], F32, name="result", tag="result", bufs=4)
-                copy = nc.vector.tensor_copy if (2 * c + half) % VECTOR_EVERY == 1 else nc.scalar.copy
-                copy(result[:], total[:])
-                rows = out[2 * half * P : 2 * (half + 1) * P, c * CHUNK : (c + 1) * CHUNK]
-                nc.sync.dma_start(out=rows.rearrange("(j p) t -> p j t", p=P), in_=result[:])
+                        second_pass(acc[:, j, :], c, 2 * half + j, r)
+                result = work.tile([P, 2, CHUNK], F32, name="result", tag="result", bufs=RESULT_BUFS)
+                copy = nc.vector.tensor_copy if half >= c else nc.scalar.copy
+                copy(result[:], acc[:])
+                stored = out[2 * half * P : 2 * (half + 1) * P, c * CHUNK : (c + 1) * CHUNK]
+                nc.sync.dma_start(out=stored.rearrange("(j p) t -> p j t", p=P), in_=result[:])
 
-        for step in range(UNITS + 3):
+        def open_last_chunk():
+            for j in range(ROW_BLOCKS):
+                if j < PRE_BANKS:
+                    last[j] = psum.tile([P, CHUNK], F32, name="last", tag="pre", bufs=PRE_BANKS)
+                else:
+                    last[j] = psum.tile([P, CHUNK], F32, name="last", tag="acc", bufs=SUM_BANKS)
+                second_pass(last[j][:], CHUNKS - 1, j, 0)
+
+        def close_last_chunk():
+            for j in range(ROW_BLOCKS):
+                second_pass(last[j][:], CHUNKS - 1, j, G - 1)
+                result = work.tile([P, CHUNK], F32, name="tail", tag="tail", bufs=ROW_BLOCKS)
+                copy = nc.scalar.copy if j % 2 == 0 else nc.vector.tensor_copy
+                copy(result[:], last[j][:])
+                nc.sync.dma_start(out=out[j * P : (j + 1) * P, T - CHUNK : T], in_=result[:])
+
+        for step in range(UNITS + QUANTIZE_LAG):
             if step < UNITS:
-                activate(step)
-            if 0 <= step - 1 < UNITS:
-                gate_and_turn(step - 1)
-            done = step - 3
+                first_product(step)
+            if 0 <= step - GATE_LAG < UNITS:
+                gate_and_turn(step - GATE_LAG)
+            done = step - QUANTIZE_LAG
             if done >= 0:
                 quantize(done)
-            if 0 <= step - 2 < UNITS:
-                regroup(step - 2)
-            if 0 <= done < UNITS - G and done % G == G - 1:
-                finish_chunk(done // G)
+            if 0 <= step - REGROUP_LAG < UNITS:
+                regroup(step - REGROUP_LAG)
+            if 0 <= step - GATE_LAG < G:
+                r = step - GATE_LAG
+                s2[r] = gather(f"s2_{r}", s2_all, list2, r, U8, f"s2_{r}")
+            if 0 <= step - REGROUP_LAG < G:
+                r = step - REGROUP_LAG
+                w2[r] = gather(f"w2_{r}", w2_all, list2, r, U32, f"w2_{r}")
             if done == UNITS - G:
-                tails = [bank([P, CHUNK], "tail", j) for j in range(ROW_BLOCKS)]
-                for j in range(ROW_BLOCKS):
-                    second_pass(tails[j][:], CHUNKS - 1, j, 0)
-
-        for j in range(ROW_BLOCKS):
-            second_pass(tails[j][:], CHUNKS - 1, j, G - 1)
-            result = work.tile([P, CHUNK], F32, name="last_result", tag="last_result", bufs=ROW_BLOCKS)
-            copy = nc.vector.tensor_copy if j % 2 == 0 else nc.scalar.copy
-            copy(result[:], tails[j][:])
-            nc.sync.dma_start(out=out[j * P : (j + 1) * P, T - CHUNK : T], in_=result[:])
+                open_last_chunk()
+            elif done == UNITS - 1:
+                close_last_chunk()
+            elif done >= 0 and done % G == G - 1:
+                second_product(done // G)

from contextlib import ExitStack

import concourse.mybir as mybir
from concourse.masks import make_identity

K, T, E, G, H, N = 512, 1024, 8, 2, 512, 512
P = 128
PACK = 4
LIST_ROWS = 16
FLOPS = 2 * T * G * (K * H + H * N)
BYTES = (K + K // 32) * (T + E * H + E * N) + 4 * G * T + 2 * P * G * (H + N) // LIST_ROWS + 4 * N * T

F32 = mybir.dt.float32
BF16 = mybir.dt.bfloat16
I32 = mybir.dt.int32
U32 = mybir.dt.uint32
U16 = mybir.dt.uint16
U8 = mybir.dt.uint8
FP8X4 = mybir.dt.float8_e4m3fn_x4

TILES = T // P
PAIR = 2
CHUNK = PAIR * P
CHUNKS = T // CHUNK
UNITS = CHUNKS * G
ROW_BLOCKS = N // P
W1_ROW, X_ROW, W2_ROW = 4, 8, 12
PRE_BANKS, TURN_BANKS, SUM_BANKS = 3, 2, 3
GATE_LAG, REGROUP_LAG, QUANTIZE_LAG = 2, 3, 4
ACT_BUFS, GATED_BUFS, GROUPED_BUFS, RESULT_BUFS = 4 * PAIR, 3 * PAIR, 3, 4


def load_scales(queue, plane, scales, row):
    rows = scales[0].bitcast(I32).rearrange("(q j) c -> j q c", j=4)
    for j in range(4):
        queue.dma_start(out=plane[:].bitcast(I32)[row + j : P : 32, :], in_=rows[j])


def words_of(packed):
    return packed[0].rearrange("p c d -> p (c d)").bitcast(I32)


def tile_moe_wsel_b_silu_p_kernel(
    tc, x_words, x_scales, w1_words, w1_scales, w2_words, w2_scales, gate, offs, offs2, out
):
    nc = tc.nc
    with ExitStack() as ctx:
        keep = ctx.enter_context(tc.tile_pool(name="keep", bufs=1))
        work = ctx.enter_context(tc.tile_pool(name="work", bufs=1))
        psum = ctx.enter_context(tc.psum_pool(name="psum", bufs=1))

        list1 = keep.tile([P, G * H // LIST_ROWS], U16, name="list1")
        list2 = keep.tile([P, G * N // LIST_ROWS], U16, name="list2")
        w1_all = keep.tile([P, E * H], U32, name="w1_all", align_bytes=64)
        s1_all = keep.tile([P, E * H], U8, name="s1_all", tag="shared", align_bytes=64)
        s2_all = keep.tile([P, E * N], U8, name="s2_all", align_bytes=64)
        x_codes = keep.tile([P, T], U32, name="x_codes", align_bytes=64)
        x_plane = keep.tile([P, T], U8, name="x_plane", align_bytes=64)
        gate_rows = keep.tile([P, P], F32, name="gate_rows", tag="early", align_bytes=64)
        gate_cols = keep.tile([P, G * TILES], F32, name="gate_cols", align_bytes=64)
        ident = keep.tile([P, P], F32, name="ident", align_bytes=64)

        nc.scalar.dma_start(out=w1_all[:].bitcast(I32), in_=words_of(w1_words))
        nc.scalar.dma_start(out=x_codes[:].bitcast(I32), in_=words_of(x_words))
        nc.sync.dma_start(list1[:], offs)
        nc.sync.dma_start(list2[:], offs2)
        nc.vector.memset(s1_all[:].bitcast(I32), 0)
        nc.vector.memset(s2_all[:].bitcast(I32), 0)
        load_scales(nc.sync, s1_all, w1_scales, W1_ROW)
        nc.gpsimd.memset(gate_rows[:], 0.0)
        make_identity(nc, ident[:])
        gate_runs = gate.rearrange("r p (m t) -> (r p m) t", t=P)
        nc.gpsimd.dma_start(out=gate_rows[0 : G * TILES, :], in_=gate_runs[0 : G * P * TILES : P + 1, :])
        load_scales(nc.gpsimd, x_plane, x_scales, X_ROW)
        load_scales(nc.sync, s2_all, w2_scales, W2_ROW)

        def gather(name, window, offsets, r, dtype, tag):
            picked = keep.tile([P, H], dtype, name=name, tag=tag, align_bytes=64)
            cols = H // LIST_ROWS
            nc.vector.tensor_copy(picked[:], window[:].indirect(offsets[:, r * cols : (r + 1) * cols]))
            return picked

        s1 = [gather(f"s1_{r}", s1_all, list1, r, U8, f"s1_{r}") for r in range(G)]

        gate_turned = psum.tile([P, 2 * PAIR, P], F32, name="gate_turned", tag="turn", bufs=TURN_BANKS)
        nc.tensor.transpose(gate_turned[:, 0, :], gate_rows[:], ident[:])
        nc.vector.tensor_copy(gate_cols[:], gate_turned[:, 0, 0 : G * TILES])

        w2_all = keep.tile([P, E * N], U32, name="w2_all", tag="early", align_bytes=64)
        nc.sync.dma_start(out=w2_all[:].bitcast(I32), in_=words_of(w2_words))

        w1 = [gather(f"w1_{r}", w1_all, list1, r, U32, "shared" if r == 0 else f"w1_{r}") for r in range(G)]

        acts, turned, grouped, codes, planes, w2, s2, last = {}, {}, {}, {}, {}, {}, {}, {}

        def first_product(u):
            c, r = divmod(u, G)
            for a in range(PAIR):
                tokens = slice((c * PAIR + a) * P, (c * PAIR + a + 1) * P)
                pre = psum.tile([P, H], F32, name="pre", tag="pre", bufs=PRE_BANKS)
                nc.tensor.matmul_mx(
                    out=pre[:],
                    lhsT=x_codes[:, tokens].bitcast(FP8X4),
                    lhsT_scale=x_plane[X_ROW:P, tokens],
                    rhs=w1[r][:].bitcast(FP8X4),
                    rhs_scale=s1[r][W1_ROW:P, :],
                    start=True,
                    stop=True,
                )
                acts[u, a] = work.tile([P, H], F32, name="act", tag="act", bufs=ACT_BUFS)
                nc.scalar.activation(
                    out=acts[u, a][:].rearrange("t (v p e) -> t v p e", v=2, e=2),
                    in_=pre[:].rearrange("t (p v e) -> t v p e", v=2, e=2),
                    func=mybir.ActivationFunctionType.Silu,
                )

        def gate_and_turn(u):
            c, r = divmod(u, G)
            turned[u] = psum.tile([P, 2 * PAIR, P], F32, name="turned", tag="turn", bufs=TURN_BANKS)
            gated = []
            for a in range(PAIR):
                col = r * TILES + c * PAIR + a
                gated.append(work.tile([P, H], BF16, name="gated", tag="gated", bufs=GATED_BUFS, align_bytes=64))
                nc.vector.tensor_scalar(
                    gated[a][:], acts[u, a][:], gate_cols[:, col : col + 1], None, mybir.AluOpType.mult
                )
            for a in range(PAIR):
                pairs = gated[a][:].bitcast(F32)
                for v in range(2):
                    nc.tensor.transpose(turned[u][:, 2 * a + v, :], pairs[:, v * P : (v + 1) * P], ident[:])

        def regroup(u):
            grouped[u] = work.tile(
                [P, CHUNK * PACK], BF16, name="grouped", tag="grouped", bufs=GROUPED_BUFS, align_bytes=64
            )
            nc.scalar.copy(
                grouped[u][:].bitcast(F32).rearrange("p (a t v) -> p a t v", a=PAIR, v=2),
                turned[u][:].rearrange("p (a v) t -> p a t v", v=2),
            )

        def quantize(u):
            codes[u] = work.tile([P, CHUNK], U32, name="codes", tag="codes", bufs=UNITS, align_bytes=64)
            planes[u] = work.tile([P, CHUNK], U8, name="planes", tag="planes", bufs=UNITS, align_bytes=64)
            nc.vector.quantize_mx(out=codes[u][:].bitcast(FP8X4), scales=planes[u][:], in_=grouped[u][:])

        def second_pass(acc, c, j, r):
            rows = slice(j * P, (j + 1) * P)
            nc.tensor.matmul_mx(
                out=acc,
                lhsT=w2[r][:, rows].bitcast(FP8X4),
                lhsT_scale=s2[r][W2_ROW:P, rows],
                rhs=codes[G * c + r][:].bitcast(FP8X4),
                rhs_scale=planes[G * c + r][:],
                start=(r == 0),
                stop=(r == G - 1),
            )

        def second_product(c):
            for half in range(2):
                acc = psum.tile([P, 2, CHUNK], F32, name="acc", tag="acc", bufs=SUM_BANKS)
                for j in range(2):
                    for r in range(G):
                        second_pass(acc[:, j, :], c, 2 * half + j, r)
                result = work.tile([P, 2, CHUNK], F32, name="result", tag="result", bufs=RESULT_BUFS)
                copy = nc.vector.tensor_copy if half >= c else nc.scalar.copy
                copy(result[:], acc[:])
                stored = out[2 * half * P : 2 * (half + 1) * P, c * CHUNK : (c + 1) * CHUNK]
                nc.sync.dma_start(out=stored.rearrange("(j p) t -> p j t", p=P), in_=result[:])

        def open_last_chunk():
            for j in range(ROW_BLOCKS):
                if j < PRE_BANKS:
                    last[j] = psum.tile([P, CHUNK], F32, name="last", tag="pre", bufs=PRE_BANKS)
                else:
                    last[j] = psum.tile([P, CHUNK], F32, name="last", tag="acc", bufs=SUM_BANKS)
                second_pass(last[j][:], CHUNKS - 1, j, 0)

        def close_last_chunk():
            for j in range(ROW_BLOCKS):
                second_pass(last[j][:], CHUNKS - 1, j, G - 1)
                result = work.tile([P, CHUNK], F32, name="tail", tag="tail", bufs=ROW_BLOCKS)
                copy = nc.scalar.copy if j % 2 == 0 else nc.vector.tensor_copy
                copy(result[:], last[j][:])
                nc.sync.dma_start(out=out[j * P : (j + 1) * P, T - CHUNK : T], in_=result[:])

        for step in range(UNITS + QUANTIZE_LAG):
            if step < UNITS:
                first_product(step)
            if 0 <= step - GATE_LAG < UNITS:
                gate_and_turn(step - GATE_LAG)
            done = step - QUANTIZE_LAG
            if done >= 0:
                quantize(done)
            if 0 <= step - REGROUP_LAG < UNITS:
                regroup(step - REGROUP_LAG)
            if 0 <= step - GATE_LAG < G:
                r = step - GATE_LAG
                s2[r] = gather(f"s2_{r}", s2_all, list2, r, U8, f"s2_{r}")
            if 0 <= step - REGROUP_LAG < G:
                r = step - REGROUP_LAG
                w2[r] = gather(f"w2_{r}", w2_all, list2, r, U32, f"w2_{r}")
            if done == UNITS - G:
                open_last_chunk()
            elif done == UNITS - 1:
                close_last_chunk()
            elif done >= 0 and done % G == G - 1:
                second_product(done // G)
